import numpy as np
import ml_dtypes


def mxq(x, axis, fmt="e4m3"):
    dtype, down = {"e4m3": (ml_dtypes.float8_e4m3fn, 7), "e5m2": (ml_dtypes.float8_e5m2, 14)}[fmt]
    v = np.moveaxis(np.asarray(x, np.float32).astype(ml_dtypes.bfloat16).astype(np.float64), axis, -1)
    blocks = v.reshape(v.shape[:-1] + (-1, 32))
    amax = np.abs(blocks).max(-1, keepdims=True)
    byte = np.maximum(np.where(amax > 0, np.frexp(amax)[1] - 1 + 127, 0) - down, 1)
    scale = np.exp2(byte - 127.0)
    codes = (blocks / scale).astype(np.float32).astype(dtype).astype(np.float64)
    return np.moveaxis((codes * scale).reshape(v.shape), -1, axis)


WIDE = False


def mx_kscale(k, group=512):
    if not WIDE:
        return np.ones(k)
    levels = np.array([10, -10, 5, -5, 0])
    if group != 512:
        return np.exp2(np.random.permutation(np.resize(levels, k // group))).repeat(group)
    if k % 512:
        return np.exp2(np.random.permutation(np.resize(levels, k // 32))).repeat(32)
    a = np.empty((k // 512, 16))
    for p in range(k // 512):
        a[p, :8] = np.random.permutation(np.resize(levels, 8))
        for g in range(8):
            far = levels[np.abs(levels - a[p, g]) >= 10]
            a[p, g + 8] = far[np.random.randint(len(far))]
    return np.exp2(a.ravel()).repeat(32)


def f64(x):
    return np.asarray(x).astype(np.float64)


def striped(idx):
    return np.tile(np.asarray(idx).reshape(-1, 16).T, (8, 1)).astype(np.uint16)


def unstriped(offs):
    return offs[:16].T.reshape(-1).astype(np.int64)


H, KV, D, NQ, N = 4, 4, 128, 512, 512
CAP = 2.0


def setup_inputs():
    n = np.random.standard_normal
    s = mx_kscale(D, 0)[:, None]
    u = mx_kscale(N)
    t = np.random.uniform(0.5, 2.0, N) * u
    v = n((KV, N, 128))
    return {
        "qT": (n((H, D, NQ)) * s * (0.70 / np.sqrt(D))).astype(np.float32),
        "kT": (n((KV, D, N)) / s).astype(np.float32),
        "t": t.reshape(N, 1).astype(np.float32),
        "v": (v / t[:, None]).astype(np.float32),
        "mask": (np.arange(N)[:, None] <= np.sort(np.random.randint(N // 4, N, NQ))[None, :]).astype(np.float32),
        "gn": np.tile(np.random.uniform(0.5, 2.0, 128), (128, 1)).astype(np.float32),
    }


def reference(qT, kT, t, v, mask, gn):
    a = mxq(f64(kT), 1, "e4m3").transpose(0, 2, 1) @ mxq(f64(qT), 1, "e4m3")
    a = CAP * np.tanh(a / CAP)
    p = a / (1.0 + np.exp(-a))
    p = p * f64(mask)
    w = p * f64(t)
    y = mxq(w, 1, "e4m3").transpose(0, 2, 1) @ mxq(f64(v), 1, "e4m3")
    y = y / 16.0
    y = y / np.sqrt(np.mean(np.square(y), -1, keepdims=True) + 1e-5) * f64(gn)[:1]
    return y

@@ -1,0 +1,302 @@
+from contextlib import ExitStack
+
+import concourse.mybir as mybir
+
+F32 = mybir.dt.float32
+BF16 = mybir.dt.bfloat16
+U32 = mybir.dt.uint32
+U8 = mybir.dt.uint8
+FP8X4 = mybir.dt.float8_e4m3fn_x4
+ACT = mybir.ActivationFunctionType
+ALU = mybir.AluOpType
+
+H, D, NQ, N, E = 4, 128, 512, 512, 128
+P = 128
+PACK = 4
+ROWS = D // PACK
+QC = 128
+CHUNKS = NQ // QC
+CAP = 2.0
+FLOPS = 2 * H * NQ * N * (D + E)
+
+
+def tile_rows_a_silu_mask_cap_onorm_kernel(tc, qT, kT, t, v, mask, gn, out):
+    nc = tc.nc
+    with ExitStack() as ctx:
+        sb = ctx.enter_context(tc.tile_pool(name="sb", bufs=1))
+        ps = ctx.enter_context(tc.psum_pool(name="ps", bufs=1))
+        ctx.enter_context(tc.manual_schedule())
+
+        def sbt(name, shape, dtype):
+            return sb.tile(shape, dtype, name=name, align_bytes=64)
+
+        q_hbm = qT.rearrange("h (p j) q -> (h p) j q", j=PACK)
+        m_hbm = mask.rearrange("(p r) q -> p r q", r=PACK)
+        k_raw = sbt("k_raw", [P, PACK, N], F32)
+        q_raw0 = sbt("q_raw0", [P, PACK, QC], F32)
+        q_raw1 = sbt("q_raw1", [P, PACK, NQ - QC], F32)
+        m_raw = [sbt("m_raw%d" % i, [P, PACK, 2 * QC], F32) for i in range(2)]
+        v_raw = sbt("v_raw", [P, H, PACK * E], F32)
+        t_sb = sbt("t_sb", [P, PACK], F32)
+        gn_sb = sbt("gn_sb", [P, E], F32)
+        nc.sync.dma_start(out=k_raw[:], in_=kT.rearrange("h (p j) n -> (h p) j n", j=PACK))
+        nc.sync.dma_start(out=q_raw0[:], in_=q_hbm[:, :, 0:QC])
+        nc.sync.dma_start(out=t_sb[:], in_=t.rearrange("(p r) o -> p (r o)", r=PACK))
+        nc.sync.dma_start(out=m_raw[0][:], in_=m_hbm[:, :, 0 : 2 * QC])
+        nc.sync.dma_start(out=q_raw1[:], in_=q_hbm[:, :, QC:NQ])
+        nc.sync.dma_start(out=v_raw[:], in_=v.rearrange("h (p r) e -> p h (r e)", r=PACK))
+        nc.sync.dma_start(out=m_raw[1][:], in_=m_hbm[:, :, 2 * QC : NQ])
+        nc.sync.dma_start(out=gn_sb[:], in_=gn)
+
+        zero_in = sbt("zero_in", [P, 1], F32)
+        zero = sbt("zero", [P, 1], F32)
+        minus_half = sbt("minus_half", [P, H], F32)
+        nc.gpsimd.memset(zero_in[:], 0.0)
+        nc.gpsimd.memset(minus_half[:], -0.5)
+        nc.scalar.activation(out=zero[:], in_=zero_in[:], func=ACT.Silu)
+
+        k_bf = [sbt("k_bf%d" % i, [P, 2, P, PACK], BF16) for i in range(2)]
+        k_codes = sbt("k_codes", [P, N], U32)
+        k_scales = sbt("k_scales", [P, N], U8)
+        q_bf0 = sbt("q_bf0", [P, QC, PACK], BF16)
+        q_bf1 = sbt("q_bf1", [P, NQ - QC, PACK], BF16)
+        q_codes = sbt("q_codes", [P, NQ], U32)
+        q_scales = sbt("q_scales", [P, NQ], U8)
+        v_bf = sbt("v_bf", [P, H, E, PACK], BF16)
+        v_codes = sbt("v_codes", [P, H * E], U32)
+        v_scales = sbt("v_scales", [P, H * E], U8)
+        mt = [sbt("mt%d" % c, [P, QC, PACK], F32) for c in range(CHUNKS)]
+        pairs = H * CHUNKS // 2
+        th = [sbt("th%d" % j, [P, 2, QC * PACK], F32) for j in range(pairs)]
+        pw = [sbt("pw%d" % j, [P, 2, QC * PACK], F32) for j in range(pairs)]
+        w_bf = [sbt("w_bf%d" % j, [P, 2, QC * PACK], BF16) for j in range(pairs)]
+        w_codes = [sbt("w_codes%d" % j, [P, 2 * QC], U32) for j in range(pairs)]
+        w_scales = [sbt("w_scales%d" % j, [P, 2 * QC], U8) for j in range(pairs)]
+        squares = sbt("squares", [P, E], BF16)
+        ssq = sbt("ssq", [P, H * CHUNKS], F32)
+        msq = sbt("msq", [P, H * CHUNKS], F32)
+        rstd = sbt("rstd", [P, H * CHUNKS], F32)
+        o_sb = [sbt("o_sb%d" % c, [P, H, E], F32) for c in range(CHUNKS)]
+        s_ps = [ps.tile([P, PACK, QC], F32, name="s_ps%d" % g) for g in range(H)]
+        y_ps = [ps.tile([P, CHUNKS, E], F32, name="y_ps%d" % g) for g in range(H)]
+
+        def quantize(codes, scales, values):
+            nc.vector.quantize_mx(out=codes.bitcast(FP8X4), scales=scales, in_=values)
+
+        def k_views(i):
+            src = k_raw[:].rearrange("p j (s r) -> p s j r", r=PACK)[:, :, :, 2 * i : 2 * i + 2]
+            return k_bf[i][:].rearrange("p r s j -> p s j r"), src
+
+        def k_quantize(i):
+            cols = slice(2 * P * i, 2 * P * (i + 1))
+            quantize(k_codes[:, cols], k_scales[:, cols], k_bf[i][:].rearrange("p r s j -> p (r s j)"))
+
+        def q_round(dst, src):
+            nc.vector.tensor_copy(
+                out=dst[:].rearrange("p (c i) j -> p c j i", i=4), in_=src[:].rearrange("p j (c i) -> p c j i", i=4)
+            )
+
+        def mask_scale(c):
+            src = m_raw[c // 2][:, :, QC * (c % 2) : QC * (c % 2 + 1)]
+            nc.vector.tensor_tensor(
+                out=mt[c][:].rearrange("p (c i) r -> p c r i", i=2),
+                in0=src.rearrange("p r (c i) -> p c r i", i=2),
+                in1=t_sb[:].unsqueeze(1).unsqueeze(3).to_broadcast([P, QC // 2, PACK, 2]),
+                op=ALU.mult,
+            )
+
+        def scores(u):
+            c, g = divmod(u, H)
+            rows = slice(ROWS * g, ROWS * (g + 1))
+            qs = slice(QC * c, QC * (c + 1))
+            for r in range(PACK):
+                ks = slice(P * r, P * (r + 1))
+                nc.tensor.matmul_mx(
+                    out=s_ps[g][:, r, :],
+                    lhsT=k_codes[rows, ks].bitcast(FP8X4),
+                    lhsT_scale=k_scales[rows, ks],
+                    rhs=q_codes[rows, qs].bitcast(FP8X4),
+                    rhs_scale=q_scales[rows, qs],
+                    start=True,
+                    stop=True,
+                )
+
+        def cap(u):
+            nc.scalar.activation(
+                out=th[u // 2][:, u % 2, :].rearrange("p (q r) -> p q r", r=PACK),
+                in_=s_ps[u % H][:].rearrange("p r q -> p q r"),
+                func=ACT.Tanh,
+                scale=1.0 / CAP,
+                bias=zero[:],
+            )
+            if u + H < H * CHUNKS:
+                scores(u + H)
+
+        def silu(u, n):
+            part = slice(u % 2, u % 2 + n)
+            nc.scalar.activation(out=pw[u // 2][:, part, :], in_=th[u // 2][:, part, :], func=ACT.Silu, scale=CAP)
+
+        def weigh(u, n):
+            part = slice(u % 2, u % 2 + n)
+            nc.vector.tensor_tensor(
+                out=w_bf[u // 2][:, part, :],
+                in0=pw[u // 2][:, part, :],
+                in1=mt[u // H][:].rearrange("p q r -> p (q r)").unsqueeze(1).to_broadcast([P, n, QC * PACK]),
+                op=ALU.mult,
+            )
+
+        def w_quantize(u, n):
+            cols = slice(QC * (u % 2), QC * (u % 2 + n))
+            quantize(
+                w_codes[u // 2][:, cols],
+                w_scales[u // 2][:, cols],
+                w_bf[u // 2][:, u % 2 : u % 2 + n, :].rearrange("p u x -> p (u x)"),
+            )
+
+        def values(u):
+            c, g = divmod(u, H)
+            cols = slice(QC * (u % 2), QC * (u % 2 + 1))
+            es = slice(E * g, E * (g + 1))
+            nc.tensor.matmul_mx(
+                out=y_ps[g][:, c, :],
+                lhsT=w_codes[u // 2][:, cols].bitcast(FP8X4),
+                lhsT_scale=w_scales[u // 2][:, cols],
+                rhs=v_codes[:, es].bitcast(FP8X4),
+                rhs_scale=v_scales[:, es],
+                start=True,
+                stop=True,
+            )
+
+        def square_sum(u):
+            c, g = divmod(u, H)
+            nc.scalar.activation(out=squares[:], in_=y_ps[g][:, c, :], func=ACT.Square, accum_out=ssq[:, u : u + 1])
+
+        def inverse_root(u, n):
+            cols = slice(u, u + n)
+            nc.gpsimd.tensor_scalar(
+                out=msq[:, cols], in0=ssq[:, cols], scalar1=1.0 / E, scalar2=256 * 1e-5, op0=ALU.mult, op1=ALU.add
+            )
+            nc.gpsimd.tensor_tensor(out=rstd[:, cols], in0=msq[:, cols], in1=minus_half[:, 0:n], op=ALU.pow)
+
+        def normalise(u):
+            c, g = divmod(u, H)
+            nc.vector.scalar_tensor_tensor(
+                out=o_sb[c][:, g, :],
+                in0=y_ps[g][:, c, :],
+                scalar=rstd[:, u : u + 1],
+                in1=gn_sb[:],
+                op0=ALU.mult,
+                op1=ALU.mult,
+            )
+
+        def store(u, n):
+            c, g = divmod(u, H)
+            nc.sync.dma_start(
+                out=out[g : g + n, QC * c : QC * (c + 1), :].rearrange("h q e -> q h e"), in_=o_sb[c][:, g : g + n, :]
+            )
+
+        def stats(c):
+            for u in range(H * c, H * (c + 1)):
+                square_sum(u)
+            inverse_root(H * c, H)
+
+        def finish(c):
+            for u in range(H * c, H * (c + 1)):
+                normalise(u)
+            store(H * c, H)
+
+        dst, src = k_views(0)
+        nc.vector.tensor_copy(out=dst, in_=src)
+        dst, src = k_views(1)
+        nc.scalar.copy(out=dst, in_=src)
+        k_quantize(0)
+        q_round(q_bf0, q_raw0)
+        k_quantize(1)
+        quantize(q_codes[:, 0:QC], q_scales[:, 0:QC], q_bf0[:].rearrange("p q j -> p (q j)"))
+        for u in range(H):
+            scores(u)
+        mask_scale(0)
+        mask_scale(1)
+        q_round(q_bf1, q_raw1)
+        flat = q_bf1[:].rearrange("p q j -> p (q j)")
+        quantize(q_codes[:, QC : 2 * QC], q_scales[:, QC : 2 * QC], flat[:, 0 : QC * PACK])
+        quantize(q_codes[:, 2 * QC : NQ], q_scales[:, 2 * QC : NQ], flat[:, QC * PACK : 3 * QC * PACK])
+
+        cap(0)
+        cap(1)
+        cap(2)
+        silu(0, 2)
+        weigh(0, 2)
+        nc.vector.tensor_copy(
+            out=v_bf[:].rearrange("p h (c i) r -> p h c r i", i=4),
+            in_=v_raw[:].rearrange("p h (r c i) -> p h c r i", r=PACK, i=4),
+        )
+        w_quantize(0, 2)
+        cap(3)
+        cap(4)
+        silu(2, 2)
+        weigh(2, 2)
+        quantize(v_codes[:], v_scales[:], v_bf[:].rearrange("p h e r -> p (h e r)"))
+        w_quantize(2, 2)
+        cap(5)
+        cap(6)
+        silu(4, 2)
+        weigh(4, 2)
+        mask_scale(2)
+        w_quantize(4, 2)
+        cap(7)
+        for u in range(0, 4):
+            values(u)
+        cap(8)
+        silu(6, 2)
+        stats(0)
+        weigh(6, 2)
+        mask_scale(3)
+        w_quantize(6, 2)
+        cap(9)
+        cap(10)
+        silu(8, 2)
+        weigh(8, 2)
+        finish(0)
+        w_quantize(8, 2)
+        cap(11)
+        for u in range(4, 8):
+            values(u)
+        cap(12)
+        silu(10, 2)
+        stats(1)
+        weigh(10, 2)
+        finish(1)
+        w_quantize(10, 2)
+        for u in range(8, 12):
+            values(u)
+        cap(13)
+        cap(14)
+        silu(12, 2)
+        cap(15)
+        silu(14, 1)
+        silu(15, 1)
+        stats(2)
+        weigh(12, 2)
+        weigh(14, 1)
+        w_quantize(12, 2)
+        values(12)
+        values(13)
+        weigh(15, 1)
+        w_quantize(14, 1)
+        values(14)
+        w_quantize(15, 1)
+        values(15)
+        finish(2)
+        square_sum(12)
+        square_sum(13)
+        inverse_root(12, 2)
+        square_sum(14)
+        square_sum(15)
+        inverse_root(14, 2)
+        normalise(12)
+        normalise(13)
+        store(12, 2)
+        normalise(14)
+        normalise(15)
+        store(14, 2)

@@ -50,9 +50,7 @@ def tile_rows_a_silu_mask_cap_onorm_kernel(tc, qT, kT, t, v, mask, gn, out):
 
         zero_in = sbt("zero_in", [P, 1], F32)
         zero = sbt("zero", [P, 1], F32)
-        minus_half = sbt("minus_half", [P, H], F32)
-        nc.gpsimd.memset(zero_in[:], 0.0)
-        nc.gpsimd.memset(minus_half[:], -0.5)
+        nc.vector.memset(zero_in[:], 0.0)
         nc.scalar.activation(out=zero[:], in_=zero_in[:], func=ACT.Silu)
 
         k_bf = [sbt("k_bf%d" % i, [P, 2, P, PACK], BF16) for i in range(2)]
@@ -74,11 +72,14 @@ def tile_rows_a_silu_mask_cap_onorm_kernel(tc, qT, kT, t, v, mask, gn, out):
         w_scales = [sbt("w_scales%d" % j, [P, 2 * QC], U8) for j in range(pairs)]
         squares = sbt("squares", [P, E], BF16)
         ssq = sbt("ssq", [P, H * CHUNKS], F32)
-        msq = sbt("msq", [P, H * CHUNKS], F32)
+        bn = sbt("bn", [P, 2 * H, 6], F32)
+        mean_sq = sbt("mean_sq", [P, 2 * H, 2], F32)
+        half_ssq = sbt("half_ssq", [P, 2 * H, 2], F32)
+        ssq_v = sbt("ssq_v", [P, 2 * H], F32)
         rstd = sbt("rstd", [P, H * CHUNKS], F32)
         o_sb = [sbt("o_sb%d" % c, [P, H, E], F32) for c in range(CHUNKS)]
         s_ps = [ps.tile([P, PACK, QC], F32, name="s_ps%d" % g) for g in range(H)]
-        y_ps = [ps.tile([P, CHUNKS, E], F32, name="y_ps%d" % g) for g in range(H)]
+        y_ps = [ps.tile([P, H, E], F32, name="y_ps%d" % c) for c in range(CHUNKS)]
 
         def quantize(codes, scales, values):
             nc.vector.quantize_mx(out=codes.bitcast(FP8X4), scales=scales, in_=values)
@@ -158,7 +159,7 @@ def tile_rows_a_silu_mask_cap_onorm_kernel(tc, qT, kT, t, v, mask, gn, out):
             cols = slice(QC * (u % 2), QC * (u % 2 + 1))
             es = slice(E * g, E * (g + 1))
             nc.tensor.matmul_mx(
-                out=y_ps[g][:, c, :],
+                out=y_ps[c][:, g, :],
                 lhsT=w_codes[u // 2][:, cols].bitcast(FP8X4),
                 lhsT_scale=w_scales[u // 2][:, cols],
                 rhs=v_codes[:, es].bitcast(FP8X4),
@@ -169,20 +170,36 @@ def tile_rows_a_silu_mask_cap_onorm_kernel(tc, qT, kT, t, v, mask, gn, out):
 
         def square_sum(u):
             c, g = divmod(u, H)
-            nc.scalar.activation(out=squares[:], in_=y_ps[g][:, c, :], func=ACT.Square, accum_out=ssq[:, u : u + 1])
+            nc.scalar.activation(out=squares[:], in_=y_ps[c][:, g, :], func=ACT.Square, accum_out=ssq[:, u : u + 1])
 
-        def inverse_root(u, n):
+        def inverse_root(src, u, n):
             cols = slice(u, u + n)
-            nc.gpsimd.tensor_scalar(
-                out=msq[:, cols], in0=ssq[:, cols], scalar1=1.0 / E, scalar2=256 * 1e-5, op0=ALU.mult, op1=ALU.add
+            nc.scalar.activation(
+                out=rstd[:, cols], in_=src[:, cols], func=ACT.Abs_reciprocal_sqrt, scale=1.0 / E, bias=256 * 1e-5
             )
-            nc.gpsimd.tensor_tensor(out=rstd[:, cols], in0=msq[:, cols], in1=minus_half[:, 0:n], op=ALU.pow)
+
+        def moments(c):
+            for g in range(H):
+                nc.vector.bn_stats(out=bn[:, H * c + g, :], in_=y_ps[c][:, g, :])
+
+        bn_fields = bn[:].rearrange("p u (h k) -> p u h k", k=3)
+
+        def square_means():
+            nc.vector.tensor_tensor(out=mean_sq[:], in0=bn_fields[:, :, :, 1], in1=bn_fields[:, :, :, 1], op=ALU.mult)
+
+        def half_sums():
+            nc.vector.scalar_tensor_tensor(
+                out=half_ssq[:], in0=mean_sq[:], scalar=E / 2, in1=bn_fields[:, :, :, 2], op0=ALU.mult, op1=ALU.add
+            )
+
+        def join_halves():
+            nc.vector.tensor_tensor(out=ssq_v[:], in0=half_ssq[:, :, 0], in1=half_ssq[:, :, 1], op=ALU.add)
 
         def normalise(u):
             c, g = divmod(u, H)
             nc.vector.scalar_tensor_tensor(
                 out=o_sb[c][:, g, :],
-                in0=y_ps[g][:, c, :],
+                in0=y_ps[c][:, g, :],
                 scalar=rstd[:, u : u + 1],
                 in1=gn_sb[:],
                 op0=ALU.mult,
@@ -194,11 +211,6 @@ def tile_rows_a_silu_mask_cap_onorm_kernel(tc, qT, kT, t, v, mask, gn, out):
             nc.sync.dma_start(
                 out=out[g : g + n, QC * c : QC * (c + 1), :].rearrange("h q e -> q h e"), in_=o_sb[c][:, g : g + n, :]
             )
-
-        def stats(c):
-            for u in range(H * c, H * (c + 1)):
-                square_sum(u)
-            inverse_root(H * c, H)
 
         def finish(c):
             for u in range(H * c, H * (c + 1)):
@@ -245,39 +257,40 @@ def tile_rows_a_silu_mask_cap_onorm_kernel(tc, qT, kT, t, v, mask, gn, out):
         mask_scale(2)
         w_quantize(4, 2)
         cap(7)
+        cap(8)
         for u in range(0, 4):
             values(u)
-        cap(8)
         silu(6, 2)
-        stats(0)
         weigh(6, 2)
-        mask_scale(3)
+        moments(0)
         w_quantize(6, 2)
         cap(9)
         cap(10)
         silu(8, 2)
         weigh(8, 2)
-        finish(0)
+        mask_scale(3)
         w_quantize(8, 2)
         cap(11)
         for u in range(4, 8):
             values(u)
+        values(8)
+        values(9)
         cap(12)
         silu(10, 2)
-        stats(1)
         weigh(10, 2)
-        finish(1)
+        moments(1)
         w_quantize(10, 2)
-        for u in range(8, 12):
-            values(u)
+        values(10)
+        values(11)
         cap(13)
         cap(14)
         silu(12, 2)
         cap(15)
         silu(14, 1)
         silu(15, 1)
-        stats(2)
+        square_means()
         weigh(12, 2)
+        half_sums()
         weigh(14, 1)
         w_quantize(12, 2)
         values(12)
@@ -285,15 +298,19 @@ def tile_rows_a_silu_mask_cap_onorm_kernel(tc, qT, kT, t, v, mask, gn, out):
         weigh(15, 1)
         w_quantize(14, 1)
         values(14)
+        join_halves()
         w_quantize(15, 1)
         values(15)
+        inverse_root(ssq_v, 0, 2 * H)
+        for u in range(8, 12):
+            square_sum(u)
+        inverse_root(ssq, 8, 4)
+        for u in range(12, 16):
+            square_sum(u)
+        inverse_root(ssq, 12, 4)
+        finish(0)
+        finish(1)
         finish(2)
-        square_sum(12)
-        square_sum(13)
-        inverse_root(12, 2)
-        square_sum(14)
-        square_sum(15)
-        inverse_root(14, 2)
         normalise(12)
         normalise(13)
         store(12, 2)

@@ -17,6 +17,7 @@ ROWS = D // PACK
 QC = 128
 CHUNKS = NQ // QC
 CAP = 2.0
+EPS = 256 * 1e-5
 FLOPS = 2 * H * NQ * N * (D + E)
 
 
@@ -34,18 +35,20 @@ def tile_rows_a_silu_mask_cap_onorm_kernel(tc, qT, kT, t, v, mask, gn, out):
         m_hbm = mask.rearrange("(p r) q -> p r q", r=PACK)
         k_raw = sbt("k_raw", [P, PACK, N], F32)
         q_raw0 = sbt("q_raw0", [P, PACK, QC], F32)
-        q_raw1 = sbt("q_raw1", [P, PACK, NQ - QC], F32)
+        q_raw1 = sbt("q_raw1", [P, PACK, QC], F32)
+        q_raw2 = sbt("q_raw2", [P, PACK, 2 * QC], F32)
         m_raw = [sbt("m_raw%d" % i, [P, PACK, 2 * QC], F32) for i in range(2)]
         v_raw = sbt("v_raw", [P, H, PACK * E], F32)
         t_sb = sbt("t_sb", [P, PACK], F32)
         gn_sb = sbt("gn_sb", [P, E], F32)
         nc.sync.dma_start(out=k_raw[:], in_=kT.rearrange("h (p j) n -> (h p) j n", j=PACK))
         nc.sync.dma_start(out=q_raw0[:], in_=q_hbm[:, :, 0:QC])
-        nc.sync.dma_start(out=t_sb[:], in_=t.rearrange("(p r) o -> p (r o)", r=PACK))
+        nc.scalar.dma_start(out=t_sb[:], in_=t.rearrange("(p r) o -> p (r o)", r=PACK))
+        nc.sync.dma_start(out=q_raw1[:], in_=q_hbm[:, :, QC : 2 * QC])
         nc.sync.dma_start(out=m_raw[0][:], in_=m_hbm[:, :, 0 : 2 * QC])
-        nc.sync.dma_start(out=q_raw1[:], in_=q_hbm[:, :, QC:NQ])
-        nc.sync.dma_start(out=v_raw[:], in_=v.rearrange("h (p r) e -> p h (r e)", r=PACK))
+        nc.sync.dma_start(out=q_raw2[:], in_=q_hbm[:, :, 2 * QC : NQ])
         nc.sync.dma_start(out=m_raw[1][:], in_=m_hbm[:, :, 2 * QC : NQ])
+        nc.sync.dma_start(out=v_raw[:], in_=v.rearrange("h (p r) e -> p h (r e)", r=PACK))
         nc.sync.dma_start(out=gn_sb[:], in_=gn)
 
         zero_in = sbt("zero_in", [P, 1], F32)
@@ -57,24 +60,23 @@ def tile_rows_a_silu_mask_cap_onorm_kernel(tc, qT, kT, t, v, mask, gn, out):
         k_codes = sbt("k_codes", [P, N], U32)
         k_scales = sbt("k_scales", [P, N], U8)
         q_bf0 = sbt("q_bf0", [P, QC, PACK], BF16)
-        q_bf1 = sbt("q_bf1", [P, NQ - QC, PACK], BF16)
+        q_bf1 = sbt("q_bf1", [P, QC, PACK], BF16)
+        q_bf2 = sbt("q_bf2", [P, 2 * QC, PACK], BF16)
         q_codes = sbt("q_codes", [P, NQ], U32)
         q_scales = sbt("q_scales", [P, NQ], U8)
         v_bf = sbt("v_bf", [P, H, E, PACK], BF16)
         v_codes = sbt("v_codes", [P, H * E], U32)
         v_scales = sbt("v_scales", [P, H * E], U8)
-        mt = [sbt("mt%d" % c, [P, QC, PACK], F32) for c in range(CHUNKS)]
-        pairs = H * CHUNKS // 2
-        th = [sbt("th%d" % j, [P, 2, QC * PACK], F32) for j in range(pairs)]
-        pw = [sbt("pw%d" % j, [P, 2, QC * PACK], F32) for j in range(pairs)]
-        w_bf = [sbt("w_bf%d" % j, [P, 2, QC * PACK], BF16) for j in range(pairs)]
-        w_codes = [sbt("w_codes%d" % j, [P, 2 * QC], U32) for j in range(pairs)]
-        w_scales = [sbt("w_scales%d" % j, [P, 2 * QC], U8) for j in range(pairs)]
+        mt = [sbt("mt%d" % i, [P, 2 * QC, PACK], F32) for i in range(2)]
+        th = [sbt("th%d" % c, [P, H, QC * PACK], F32) for c in range(CHUNKS)]
+        pw = [sbt("pw%d" % c, [P, H, QC * PACK], F32) for c in range(CHUNKS)]
+        w_bf = [sbt("w_bf%d" % c, [P, H, QC * PACK], BF16) for c in range(CHUNKS)]
+        w_codes = [sbt("w_codes%d" % c, [P, H * QC], U32) for c in range(CHUNKS)]
+        w_scales = [sbt("w_scales%d" % c, [P, H * QC], U8) for c in range(CHUNKS)]
         squares = sbt("squares", [P, E], BF16)
         ssq = sbt("ssq", [P, H * CHUNKS], F32)
-        bn = sbt("bn", [P, 2 * H, 6], F32)
-        mean_sq = sbt("mean_sq", [P, 2 * H, 2], F32)
-        half_ssq = sbt("half_ssq", [P, 2 * H, 2], F32)
+        bn = sbt("bn", [P, 2 * H, 3], F32)
+        mean_sq = sbt("mean_sq", [P, 2 * H], F32)
         ssq_v = sbt("ssq_v", [P, 2 * H], F32)
         rstd = sbt("rstd", [P, H * CHUNKS], F32)
         o_sb = [sbt("o_sb%d" % c, [P, H, E], F32) for c in range(CHUNKS)]
@@ -84,25 +86,22 @@ def tile_rows_a_silu_mask_cap_onorm_kernel(tc, qT, kT, t, v, mask, gn, out):
         def quantize(codes, scales, values):
             nc.vector.quantize_mx(out=codes.bitcast(FP8X4), scales=scales, in_=values)
 
-        def k_views(i):
-            src = k_raw[:].rearrange("p j (s r) -> p s j r", r=PACK)[:, :, :, 2 * i : 2 * i + 2]
-            return k_bf[i][:].rearrange("p r s j -> p s j r"), src
+        def k_views(i, s0, s1):
+            src = k_raw[:].rearrange("p j (s r) -> p s j r", r=PACK)[:, s0:s1, :, 2 * i : 2 * i + 2]
+            return k_bf[i][:, :, s0:s1, :].rearrange("p r s j -> p s j r"), src
 
-        def k_quantize(i):
-            cols = slice(2 * P * i, 2 * P * (i + 1))
-            quantize(k_codes[:, cols], k_scales[:, cols], k_bf[i][:].rearrange("p r s j -> p (r s j)"))
+        def k_quantize(r):
+            cols = slice(P * r, P * (r + 1))
+            quantize(k_codes[:, cols], k_scales[:, cols], k_bf[r // 2][:, r % 2, :, :].rearrange("p s j -> p (s j)"))
 
-        def q_round(dst, src):
-            nc.vector.tensor_copy(
-                out=dst[:].rearrange("p (c i) j -> p c j i", i=4), in_=src[:].rearrange("p j (c i) -> p c j i", i=4)
-            )
+        def q_views(dst, src):
+            return dst[:].rearrange("p (c i) j -> p c j i", i=4), src[:].rearrange("p j (c i) -> p c j i", i=4)
 
-        def mask_scale(c):
-            src = m_raw[c // 2][:, :, QC * (c % 2) : QC * (c % 2 + 1)]
+        def mask_scale(i):
             nc.vector.tensor_tensor(
-                out=mt[c][:].rearrange("p (c i) r -> p c r i", i=2),
-                in0=src.rearrange("p r (c i) -> p c r i", i=2),
-                in1=t_sb[:].unsqueeze(1).unsqueeze(3).to_broadcast([P, QC // 2, PACK, 2]),
+                out=mt[i][:].rearrange("p (c i) r -> p c r i" if i == 0 else "p (i c) r -> p c r i", i=2),
+                in0=m_raw[i][:].rearrange("p r (c i) -> p c r i", i=2),
+                in1=t_sb[:].unsqueeze(1).unsqueeze(3).to_broadcast([P, QC, PACK, 2]),
                 op=ALU.mult,
             )
 
@@ -124,7 +123,7 @@ def tile_rows_a_silu_mask_cap_onorm_kernel(tc, qT, kT, t, v, mask, gn, out):
 
         def cap(u):
             nc.scalar.activation(
-                out=th[u // 2][:, u % 2, :].rearrange("p (q r) -> p q r", r=PACK),
+                out=th[u // H][:, u % H, :].rearrange("p (q r) -> p q r", r=PACK),
                 in_=s_ps[u % H][:].rearrange("p r q -> p q r"),
                 func=ACT.Tanh,
                 scale=1.0 / CAP,
@@ -134,105 +133,110 @@ def tile_rows_a_silu_mask_cap_onorm_kernel(tc, qT, kT, t, v, mask, gn, out):
                 scores(u + H)
 
         def silu(u, n):
-            part = slice(u % 2, u % 2 + n)
-            nc.scalar.activation(out=pw[u // 2][:, part, :], in_=th[u // 2][:, part, :], func=ACT.Silu, scale=CAP)
+            c, g = divmod(u, H)
+            nc.scalar.activation(out=pw[c][:, g : g + n, :], in_=th[c][:, g : g + n, :], func=ACT.Silu, scale=CAP)
 
         def weigh(u, n):
-            part = slice(u % 2, u % 2 + n)
+            c, g = divmod(u, H)
+            factors = mt[c // 2][:, QC * (c % 2) : QC * (c % 2 + 1), :].rearrange("p q r -> p (q r)")
             nc.vector.tensor_tensor(
-                out=w_bf[u // 2][:, part, :],
-                in0=pw[u // 2][:, part, :],
-                in1=mt[u // H][:].rearrange("p q r -> p (q r)").unsqueeze(1).to_broadcast([P, n, QC * PACK]),
+                out=w_bf[c][:, g : g + n, :],
+                in0=pw[c][:, g : g + n, :],
+                in1=factors.unsqueeze(1).to_broadcast([P, n, QC * PACK]),
                 op=ALU.mult,
             )
 
         def w_quantize(u, n):
-            cols = slice(QC * (u % 2), QC * (u % 2 + n))
-            quantize(
-                w_codes[u // 2][:, cols],
-                w_scales[u // 2][:, cols],
-                w_bf[u // 2][:, u % 2 : u % 2 + n, :].rearrange("p u x -> p (u x)"),
-            )
-
-        def values(u):
             c, g = divmod(u, H)
-            cols = slice(QC * (u % 2), QC * (u % 2 + 1))
-            es = slice(E * g, E * (g + 1))
-            nc.tensor.matmul_mx(
-                out=y_ps[c][:, g, :],
-                lhsT=w_codes[u // 2][:, cols].bitcast(FP8X4),
-                lhsT_scale=w_scales[u // 2][:, cols],
-                rhs=v_codes[:, es].bitcast(FP8X4),
-                rhs_scale=v_scales[:, es],
-                start=True,
-                stop=True,
-            )
+            cols = slice(QC * g, QC * (g + n))
+            quantize(w_codes[c][:, cols], w_scales[c][:, cols], w_bf[c][:, g : g + n, :].rearrange("p u x -> p (u x)"))
 
-        def square_sum(u):
-            c, g = divmod(u, H)
-            nc.scalar.activation(out=squares[:], in_=y_ps[c][:, g, :], func=ACT.Square, accum_out=ssq[:, u : u + 1])
+        def values(u, n):
+            c = u // H
+            for g in range(u % H, u % H + n):
+                cols = slice(QC * g, QC * (g + 1))
+                es = slice(E * g, E * (g + 1))
+                nc.tensor.matmul_mx(
+                    out=y_ps[c][:, g, :] if c < 2 else y_ps[2 + g // 2][:, 2 * (g % 2) + c - 2, :],
+                    lhsT=w_codes[c][:, cols].bitcast(FP8X4),
+                    lhsT_scale=w_scales[c][:, cols],
+                    rhs=v_codes[:, es].bitcast(FP8X4),
+                    rhs_scale=v_scales[:, es],
+                    start=True,
+                    stop=True,
+                )
 
-        def inverse_root(src, u, n):
-            cols = slice(u, u + n)
+        def square_sum(b, i):
+            n = 4 * b + i
+            nc.scalar.activation(out=squares[:], in_=y_ps[b][:, i, :], func=ACT.Square, accum_out=ssq[:, n : n + 1])
+
+        def inverse_root(src, n0, n, dst0):
             nc.scalar.activation(
-                out=rstd[:, cols], in_=src[:, cols], func=ACT.Abs_reciprocal_sqrt, scale=1.0 / E, bias=256 * 1e-5
+                out=rstd[:, dst0 : dst0 + n],
+                in_=src[:, n0 : n0 + n],
+                func=ACT.Abs_reciprocal_sqrt,
+                scale=1.0 / E,
+                bias=EPS,
             )
 
         def moments(c):
-            for g in range(H):
-                nc.vector.bn_stats(out=bn[:, H * c + g, :], in_=y_ps[c][:, g, :])
-
-        bn_fields = bn[:].rearrange("p u (h k) -> p u h k", k=3)
+            for g in range(0, H, 2):
+                u = H * c + g
+                nc.vector.bn_stats(
+                    out=bn[:, u : u + 2, :].rearrange("p u k -> p (u k)"),
+                    in_=y_ps[c][:, g : g + 2, :].rearrange("p g e -> p e g"),
+                )
 
         def square_means():
-            nc.vector.tensor_tensor(out=mean_sq[:], in0=bn_fields[:, :, :, 1], in1=bn_fields[:, :, :, 1], op=ALU.mult)
+            nc.vector.tensor_tensor(out=mean_sq[:], in0=bn[:, :, 1], in1=bn[:, :, 1], op=ALU.mult)
 
-        def half_sums():
+        def join_moments():
             nc.vector.scalar_tensor_tensor(
-                out=half_ssq[:], in0=mean_sq[:], scalar=E / 2, in1=bn_fields[:, :, :, 2], op0=ALU.mult, op1=ALU.add
+                out=ssq_v[:], in0=mean_sq[:], scalar=float(E), in1=bn[:, :, 2], op0=ALU.mult, op1=ALU.add
             )
 
-        def join_halves():
-            nc.vector.tensor_tensor(out=ssq_v[:], in0=half_ssq[:, :, 0], in1=half_ssq[:, :, 1], op=ALU.add)
-
-        def normalise(u):
-            c, g = divmod(u, H)
+        def normalise(b, i):
+            n = 4 * b + i
             nc.vector.scalar_tensor_tensor(
-                out=o_sb[c][:, g, :],
-                in0=y_ps[c][:, g, :],
-                scalar=rstd[:, u : u + 1],
+                out=o_sb[b][:, i, :],
+                in0=y_ps[b][:, i, :],
+                scalar=rstd[:, n : n + 1],
                 in1=gn_sb[:],
                 op0=ALU.mult,
                 op1=ALU.mult,
             )
 
-        def store(u, n):
-            c, g = divmod(u, H)
-            nc.sync.dma_start(
-                out=out[g : g + n, QC * c : QC * (c + 1), :].rearrange("h q e -> q h e"), in_=o_sb[c][:, g : g + n, :]
-            )
+        def store(b, i0, n):
+            if b < 2:
+                dst = out[i0 : i0 + n, QC * b : QC * (b + 1), :].rearrange("h q e -> q h e")
+                src = o_sb[b][:, i0 : i0 + n, :]
+            else:
+                g0 = 2 * (b - 2) + i0 // 2
+                dst = out[g0 : g0 + n // 2, 2 * QC : NQ, :].rearrange("h (m i) e -> m h (i e)", i=2)
+                src = o_sb[b][:, i0 : i0 + n, :].rearrange("p (h i) e -> p h (i e)", i=2)
+            nc.sync.dma_start(out=dst, in_=src)
 
-        def finish(c):
-            for u in range(H * c, H * (c + 1)):
-                normalise(u)
-            store(H * c, H)
-
-        dst, src = k_views(0)
+        dst, src = k_views(0, 0, P)
         nc.vector.tensor_copy(out=dst, in_=src)
-        dst, src = k_views(1)
+        dst, src = k_views(1, 0, P)
+        nc.scalar.copy(out=dst, in_=src)
+        dst, src = q_views(q_bf0, q_raw0)
+        nc.vector.tensor_copy(out=dst, in_=src)
+        dst, src = q_views(q_bf1, q_raw1)
         nc.scalar.copy(out=dst, in_=src)
         k_quantize(0)
-        q_round(q_bf0, q_raw0)
-        k_quantize(1)
         quantize(q_codes[:, 0:QC], q_scales[:, 0:QC], q_bf0[:].rearrange("p q j -> p (q j)"))
+        for r in range(1, PACK):
+            k_quantize(r)
         for u in range(H):
             scores(u)
+        quantize(q_codes[:, QC : 2 * QC], q_scales[:, QC : 2 * QC], q_bf1[:].rearrange("p q j -> p (q j)"))
         mask_scale(0)
+        nc.vector.tensor_copy(
+            out=q_bf2[:].rearrange("p (i m) j -> p m j i", i=2), in_=q_raw2[:].rearrange("p j (m i) -> p m j i", i=2)
+        )
         mask_scale(1)
-        q_round(q_bf1, q_raw1)
-        flat = q_bf1[:].rearrange("p q j -> p (q j)")
-        quantize(q_codes[:, QC : 2 * QC], q_scales[:, QC : 2 * QC], flat[:, 0 : QC * PACK])
-        quantize(q_codes[:, 2 * QC : NQ], q_scales[:, 2 * QC : NQ], flat[:, QC * PACK : 3 * QC * PACK])
+        quantize(q_codes[:, 2 * QC : NQ], q_scales[:, 2 * QC : NQ], q_bf2[:].rearrange("p q j -> p (q j)"))
 
         cap(0)
         cap(1)
@@ -243,45 +247,35 @@ def tile_rows_a_silu_mask_cap_onorm_kernel(tc, qT, kT, t, v, mask, gn, out):
             out=v_bf[:].rearrange("p h (c i) r -> p h c r i", i=4),
             in_=v_raw[:].rearrange("p h (r c i) -> p h c r i", r=PACK, i=4),
         )
-        w_quantize(0, 2)
         cap(3)
         cap(4)
         silu(2, 2)
         weigh(2, 2)
         quantize(v_codes[:], v_scales[:], v_bf[:].rearrange("p h e r -> p (h e r)"))
-        w_quantize(2, 2)
+        w_quantize(0, 4)
         cap(5)
         cap(6)
+        values(0, 4)
         silu(4, 2)
         weigh(4, 2)
-        mask_scale(2)
-        w_quantize(4, 2)
         cap(7)
         cap(8)
-        for u in range(0, 4):
-            values(u)
         silu(6, 2)
         weigh(6, 2)
         moments(0)
-        w_quantize(6, 2)
+        w_quantize(4, 4)
         cap(9)
         cap(10)
         silu(8, 2)
         weigh(8, 2)
-        mask_scale(3)
-        w_quantize(8, 2)
         cap(11)
-        for u in range(4, 8):
-            values(u)
-        values(8)
-        values(9)
+        values(4, 4)
         cap(12)
         silu(10, 2)
         weigh(10, 2)
         moments(1)
-        w_quantize(10, 2)
-        values(10)
-        values(11)
+        w_quantize(8, 4)
+        values(8, 4)
         cap(13)
         cap(14)
         silu(12, 2)
@@ -290,30 +284,24 @@ def tile_rows_a_silu_mask_cap_onorm_kernel(tc, qT, kT, t, v, mask, gn, out):
         silu(15, 1)
         square_means()
         weigh(12, 2)
-        half_sums()
+        join_moments()
         weigh(14, 1)
         w_quantize(12, 2)
-        values(12)
-        values(13)
+        values(12, 2)
         weigh(15, 1)
         w_quantize(14, 1)
-        values(14)
-        join_halves()
+        values(14, 1)
         w_quantize(15, 1)
-        values(15)
-        inverse_root(ssq_v, 0, 2 * H)
-        for u in range(8, 12):
-            square_sum(u)
-        inverse_root(ssq, 8, 4)
-        for u in range(12, 16):
-            square_sum(u)
-        inverse_root(ssq, 12, 4)
-        finish(0)
-        finish(1)
-        finish(2)
-        normalise(12)
-        normalise(13)
-        store(12, 2)
-        normalise(14)
-        normalise(15)
-        store(14, 2)
+        values(15, 1)
+        inverse_root(ssq_v, 0, 2 * H, 0)
+        for b in (2, 3):
+            for i in range(4):
+                square_sum(b, i)
+            inverse_root(ssq, 4 * b, 4, 4 * b)
+        for b in range(4):
+            for i in range(4):
+                normalise(b, i)
+                if b in (0, 3) and i % 2 == 1:
+                    store(b, i - 1, 2)
+            if b in (1, 2):
+                store(b, 0, 4)

@@ -16,9 +16,20 @@ PACK = 4
 ROWS = D // PACK
 QC = 128
 CHUNKS = NQ // QC
+UNITS = H * CHUNKS
+BANK_UNITS = 4
 CAP = 2.0
-EPS = 256 * 1e-5
+EPS = 16 * 16 * 1e-5
 FLOPS = 2 * H * NQ * N * (D + E)
+
+GROUPS = [(u, 1) for u in range(H)] + [(u, 2) for u in range(H, UNITS - 2, 2)] + [(UNITS - 2, 1), (UNITS - 1, 1)]
+
+
+def result_place(u):
+    c, g = divmod(u, H)
+    if c < 2:
+        return c, g
+    return 2 + g // 2, 2 * (g % 2) + c - 2
 
 
 def tile_rows_a_silu_mask_cap_onorm_kernel(tc, qT, kT, t, v, mask, gn, out):
@@ -28,179 +39,200 @@ def tile_rows_a_silu_mask_cap_onorm_kernel(tc, qT, kT, t, v, mask, gn, out):
         ps = ctx.enter_context(tc.psum_pool(name="ps", bufs=1))
         ctx.enter_context(tc.manual_schedule())
 
-        def sbt(name, shape, dtype):
+        def sbuf(name, shape, dtype):
             return sb.tile(shape, dtype, name=name, align_bytes=64)
 
         q_hbm = qT.rearrange("h (p j) q -> (h p) j q", j=PACK)
-        m_hbm = mask.rearrange("(p r) q -> p r q", r=PACK)
-        k_raw = sbt("k_raw", [P, PACK, N], F32)
-        q_raw0 = sbt("q_raw0", [P, PACK, QC], F32)
-        q_raw1 = sbt("q_raw1", [P, PACK, QC], F32)
-        q_raw2 = sbt("q_raw2", [P, PACK, 2 * QC], F32)
-        m_raw = [sbt("m_raw%d" % i, [P, PACK, 2 * QC], F32) for i in range(2)]
-        v_raw = sbt("v_raw", [P, H, PACK * E], F32)
-        t_sb = sbt("t_sb", [P, PACK], F32)
-        gn_sb = sbt("gn_sb", [P, E], F32)
+        mask_hbm = mask.rearrange("(s r) q -> s r q", r=PACK)
+        k_raw = sbuf("k_raw", [P, PACK, N], F32)
+        q_raw = [sbuf("q_raw%d" % c, [P, PACK, QC], F32) for c in range(2)]
+        q_raw_late = sbuf("q_raw_late", [P, PACK, 2 * QC], F32)
+        mask_raw = [sbuf("mask_raw%d" % half, [P, PACK, 2 * QC], F32) for half in range(2)]
+        v_raw = sbuf("v_raw", [P, H, PACK * E], F32)
+        t_sb = sbuf("t_sb", [P, PACK], F32)
+        gn_sb = sbuf("gn_sb", [P, E], F32)
         nc.sync.dma_start(out=k_raw[:], in_=kT.rearrange("h (p j) n -> (h p) j n", j=PACK))
-        nc.sync.dma_start(out=q_raw0[:], in_=q_hbm[:, :, 0:QC])
-        nc.scalar.dma_start(out=t_sb[:], in_=t.rearrange("(p r) o -> p (r o)", r=PACK))
-        nc.sync.dma_start(out=q_raw1[:], in_=q_hbm[:, :, QC : 2 * QC])
-        nc.sync.dma_start(out=m_raw[0][:], in_=m_hbm[:, :, 0 : 2 * QC])
-        nc.sync.dma_start(out=q_raw2[:], in_=q_hbm[:, :, 2 * QC : NQ])
-        nc.sync.dma_start(out=m_raw[1][:], in_=m_hbm[:, :, 2 * QC : NQ])
-        nc.sync.dma_start(out=v_raw[:], in_=v.rearrange("h (p r) e -> p h (r e)", r=PACK))
+        nc.sync.dma_start(out=q_raw[0][:], in_=q_hbm[:, :, 0:QC])
+        nc.scalar.dma_start(out=t_sb[:], in_=t.rearrange("(s r) o -> s (r o)", r=PACK))
+        nc.sync.dma_start(out=q_raw[1][:], in_=q_hbm[:, :, QC : 2 * QC])
+        nc.sync.dma_start(out=mask_raw[0][:], in_=mask_hbm[:, :, 0 : 2 * QC])
+        nc.sync.dma_start(out=q_raw_late[:], in_=q_hbm[:, :, 2 * QC : NQ])
+        nc.sync.dma_start(out=mask_raw[1][:], in_=mask_hbm[:, :, 2 * QC : NQ])
+        nc.sync.dma_start(out=v_raw[:], in_=v.rearrange("h (s r) e -> s h (r e)", r=PACK))
         nc.sync.dma_start(out=gn_sb[:], in_=gn)
 
-        zero_in = sbt("zero_in", [P, 1], F32)
-        zero = sbt("zero", [P, 1], F32)
+        zero_in = sbuf("zero_in", [P, 1], F32)
+        zero_bias = sbuf("zero_bias", [P, 1], F32)
         nc.vector.memset(zero_in[:], 0.0)
-        nc.scalar.activation(out=zero[:], in_=zero_in[:], func=ACT.Silu)
+        nc.scalar.activation(out=zero_bias[:], in_=zero_in[:], func=ACT.Silu)
 
-        k_bf = [sbt("k_bf%d" % i, [P, 2, P, PACK], BF16) for i in range(2)]
-        k_codes = sbt("k_codes", [P, N], U32)
-        k_scales = sbt("k_scales", [P, N], U8)
-        q_bf0 = sbt("q_bf0", [P, QC, PACK], BF16)
-        q_bf1 = sbt("q_bf1", [P, QC, PACK], BF16)
-        q_bf2 = sbt("q_bf2", [P, 2 * QC, PACK], BF16)
-        q_codes = sbt("q_codes", [P, NQ], U32)
-        q_scales = sbt("q_scales", [P, NQ], U8)
-        v_bf = sbt("v_bf", [P, H, E, PACK], BF16)
-        v_codes = sbt("v_codes", [P, H * E], U32)
-        v_scales = sbt("v_scales", [P, H * E], U8)
-        mt = [sbt("mt%d" % i, [P, 2 * QC, PACK], F32) for i in range(2)]
-        th = [sbt("th%d" % c, [P, H, QC * PACK], F32) for c in range(CHUNKS)]
-        pw = [sbt("pw%d" % c, [P, H, QC * PACK], F32) for c in range(CHUNKS)]
-        w_bf = [sbt("w_bf%d" % c, [P, H, QC * PACK], BF16) for c in range(CHUNKS)]
-        w_codes = [sbt("w_codes%d" % c, [P, H * QC], U32) for c in range(CHUNKS)]
-        w_scales = [sbt("w_scales%d" % c, [P, H * QC], U8) for c in range(CHUNKS)]
-        squares = sbt("squares", [P, E], BF16)
-        ssq = sbt("ssq", [P, H * CHUNKS], F32)
-        bn = sbt("bn", [P, 2 * H, 3], F32)
-        mean_sq = sbt("mean_sq", [P, 2 * H], F32)
-        ssq_v = sbt("ssq_v", [P, 2 * H], F32)
-        rstd = sbt("rstd", [P, H * CHUNKS], F32)
-        o_sb = [sbt("o_sb%d" % c, [P, H, E], F32) for c in range(CHUNKS)]
+        k_bf = [sbuf("k_bf%d" % half, [P, 2, P, PACK], BF16) for half in range(2)]
+        k_codes = sbuf("k_codes", [P, N], U32)
+        k_scales = sbuf("k_scales", [P, N], U8)
+        q_bf = [sbuf("q_bf%d" % c, [P, QC, PACK], BF16) for c in range(2)]
+        q_bf_late = sbuf("q_bf_late", [P, 2 * QC, PACK], BF16)
+        q_codes = sbuf("q_codes", [P, NQ], U32)
+        q_scales = sbuf("q_scales", [P, NQ], U8)
+        v_bf = sbuf("v_bf", [P, H, E, PACK], BF16)
+        v_codes = sbuf("v_codes", [P, H * E], U32)
+        v_scales = sbuf("v_scales", [P, H * E], U8)
+        mask_t = [sbuf("mask_t%d" % half, [P, 2 * QC, PACK], F32) for half in range(2)]
+        capped = [sbuf("capped%d" % c, [P, H, QC * PACK], F32) for c in range(CHUNKS)]
+        silus = [sbuf("silus%d" % c, [P, H, QC * PACK], F32) for c in range(CHUNKS)]
+        w_bf = [sbuf("w_bf%d" % c, [P, H, QC * PACK], BF16) for c in range(CHUNKS)]
+        w_codes = [sbuf("w_codes%d" % c, [P, H * QC], U32) for c in range(CHUNKS)]
+        w_scales = [sbuf("w_scales%d" % c, [P, H * QC], U8) for c in range(CHUNKS)]
+        squares = sbuf("squares", [P, E], BF16)
+        moments = sbuf("moments", [P, 2 * BANK_UNITS, 3], F32)
+        mean_sq = sbuf("mean_sq", [P, 2 * BANK_UNITS], F32)
+        sum_sq_early = sbuf("sum_sq_early", [P, 2 * BANK_UNITS], F32)
+        sum_sq_late = sbuf("sum_sq_late", [P, UNITS], F32)
+        inv_rms = sbuf("inv_rms", [P, UNITS], F32)
+        o_sb = [sbuf("o_sb%d" % b, [P, BANK_UNITS, E], F32) for b in range(CHUNKS)]
         s_ps = [ps.tile([P, PACK, QC], F32, name="s_ps%d" % g) for g in range(H)]
-        y_ps = [ps.tile([P, H, E], F32, name="y_ps%d" % c) for c in range(CHUNKS)]
+        y_ps = [ps.tile([P, BANK_UNITS, E], F32, name="y_ps%d" % b) for b in range(CHUNKS)]
 
         def quantize(codes, scales, values):
             nc.vector.quantize_mx(out=codes.bitcast(FP8X4), scales=scales, in_=values)
 
-        def k_views(i, s0, s1):
-            src = k_raw[:].rearrange("p j (s r) -> p s j r", r=PACK)[:, s0:s1, :, 2 * i : 2 * i + 2]
-            return k_bf[i][:, :, s0:s1, :].rearrange("p r s j -> p s j r"), src
+        def round_keys(copy, half):
+            src = k_raw[:].rearrange("p j (s r) -> p s j r", r=PACK)[:, :, :, 2 * half : 2 * half + 2]
+            copy(out=k_bf[half][:].rearrange("p r s j -> p s j r"), in_=src)
 
-        def k_quantize(r):
+        def quantize_keys(r):
             cols = slice(P * r, P * (r + 1))
             quantize(k_codes[:, cols], k_scales[:, cols], k_bf[r // 2][:, r % 2, :, :].rearrange("p s j -> p (s j)"))
 
-        def q_views(dst, src):
-            return dst[:].rearrange("p (c i) j -> p c j i", i=4), src[:].rearrange("p j (c i) -> p c j i", i=4)
+        def round_queries(copy, c):
+            copy(
+                out=q_bf[c][:].rearrange("p (m x) j -> p m j x", x=4),
+                in_=q_raw[c][:].rearrange("p j (m x) -> p m j x", x=4),
+            )
 
-        def mask_scale(i):
+        def quantize_queries(c):
+            cols = slice(QC * c, QC * (c + 1))
+            quantize(q_codes[:, cols], q_scales[:, cols], q_bf[c][:].rearrange("p q j -> p (q j)"))
+
+        def round_late_queries():
+            nc.vector.tensor_copy(
+                out=q_bf_late[:].rearrange("p (x m) j -> p m j x", x=2),
+                in_=q_raw_late[:].rearrange("p j (m x) -> p m j x", x=2),
+            )
+
+        def quantize_late_queries():
+            cols = slice(2 * QC, NQ)
+            quantize(q_codes[:, cols], q_scales[:, cols], q_bf_late[:].rearrange("p q j -> p (q j)"))
+
+        def scale_mask(half):
+            order = "p (m x) r -> p m r x" if half == 0 else "p (x m) r -> p m r x"
             nc.vector.tensor_tensor(
-                out=mt[i][:].rearrange("p (c i) r -> p c r i" if i == 0 else "p (i c) r -> p c r i", i=2),
-                in0=m_raw[i][:].rearrange("p r (c i) -> p c r i", i=2),
+                out=mask_t[half][:].rearrange(order, x=2),
+                in0=mask_raw[half][:].rearrange("p r (m x) -> p m r x", x=2),
                 in1=t_sb[:].unsqueeze(1).unsqueeze(3).to_broadcast([P, QC, PACK, 2]),
                 op=ALU.mult,
             )
 
+        def round_values():
+            nc.vector.tensor_copy(
+                out=v_bf[:].rearrange("p h (m x) r -> p h m r x", x=4),
+                in_=v_raw[:].rearrange("p h (r m x) -> p h m r x", r=PACK, x=4),
+            )
+
+        def quantize_values():
+            quantize(v_codes[:], v_scales[:], v_bf[:].rearrange("p h e r -> p (h e r)"))
+
         def scores(u):
             c, g = divmod(u, H)
             rows = slice(ROWS * g, ROWS * (g + 1))
-            qs = slice(QC * c, QC * (c + 1))
+            q_cols = slice(QC * c, QC * (c + 1))
             for r in range(PACK):
-                ks = slice(P * r, P * (r + 1))
+                k_cols = slice(P * r, P * (r + 1))
                 nc.tensor.matmul_mx(
                     out=s_ps[g][:, r, :],
-                    lhsT=k_codes[rows, ks].bitcast(FP8X4),
-                    lhsT_scale=k_scales[rows, ks],
-                    rhs=q_codes[rows, qs].bitcast(FP8X4),
-                    rhs_scale=q_scales[rows, qs],
+                    lhsT=k_codes[rows, k_cols].bitcast(FP8X4),
+                    lhsT_scale=k_scales[rows, k_cols],
+                    rhs=q_codes[rows, q_cols].bitcast(FP8X4),
+                    rhs_scale=q_scales[rows, q_cols],
                     start=True,
                     stop=True,
                 )
 
         def cap(u):
+            c, g = divmod(u, H)
             nc.scalar.activation(
-                out=th[u // H][:, u % H, :].rearrange("p (q r) -> p q r", r=PACK),
-                in_=s_ps[u % H][:].rearrange("p r q -> p q r"),
+                out=capped[c][:, g, :].rearrange("p (q r) -> p q r", r=PACK),
+                in_=s_ps[g][:].rearrange("p r q -> p q r"),
                 func=ACT.Tanh,
                 scale=1.0 / CAP,
-                bias=zero[:],
+                bias=zero_bias[:],
             )
-            if u + H < H * CHUNKS:
+            if u + H < UNITS:
                 scores(u + H)
 
         def silu(u, n):
             c, g = divmod(u, H)
-            nc.scalar.activation(out=pw[c][:, g : g + n, :], in_=th[c][:, g : g + n, :], func=ACT.Silu, scale=CAP)
+            nc.scalar.activation(
+                out=silus[c][:, g : g + n, :], in_=capped[c][:, g : g + n, :], func=ACT.Silu, scale=CAP
+            )
 
         def weigh(u, n):
             c, g = divmod(u, H)
-            factors = mt[c // 2][:, QC * (c % 2) : QC * (c % 2 + 1), :].rearrange("p q r -> p (q r)")
+            factors = mask_t[c // 2][:, QC * (c % 2) : QC * (c % 2 + 1), :].rearrange("p q r -> p (q r)")
             nc.vector.tensor_tensor(
                 out=w_bf[c][:, g : g + n, :],
-                in0=pw[c][:, g : g + n, :],
+                in0=silus[c][:, g : g + n, :],
                 in1=factors.unsqueeze(1).to_broadcast([P, n, QC * PACK]),
                 op=ALU.mult,
             )
 
-        def w_quantize(u, n):
+        def quantize_weights(u, n):
             c, g = divmod(u, H)
             cols = slice(QC * g, QC * (g + n))
-            quantize(w_codes[c][:, cols], w_scales[c][:, cols], w_bf[c][:, g : g + n, :].rearrange("p u x -> p (u x)"))
+            quantize(w_codes[c][:, cols], w_scales[c][:, cols], w_bf[c][:, g : g + n, :].rearrange("p g x -> p (g x)"))
 
-        def values(u, n):
-            c = u // H
-            for g in range(u % H, u % H + n):
-                cols = slice(QC * g, QC * (g + 1))
-                es = slice(E * g, E * (g + 1))
+        def results(u0, n):
+            for u in range(u0, u0 + n):
+                c, g = divmod(u, H)
+                b, i = result_place(u)
+                q_cols = slice(QC * g, QC * (g + 1))
+                e_cols = slice(E * g, E * (g + 1))
                 nc.tensor.matmul_mx(
-                    out=y_ps[c][:, g, :] if c < 2 else y_ps[2 + g // 2][:, 2 * (g % 2) + c - 2, :],
-                    lhsT=w_codes[c][:, cols].bitcast(FP8X4),
-                    lhsT_scale=w_scales[c][:, cols],
-                    rhs=v_codes[:, es].bitcast(FP8X4),
-                    rhs_scale=v_scales[:, es],
+                    out=y_ps[b][:, i, :],
+                    lhsT=w_codes[c][:, q_cols].bitcast(FP8X4),
+                    lhsT_scale=w_scales[c][:, q_cols],
+                    rhs=v_codes[:, e_cols].bitcast(FP8X4),
+                    rhs_scale=v_scales[:, e_cols],
                     start=True,
                     stop=True,
                 )
 
-        def square_sum(b, i):
-            n = 4 * b + i
-            nc.scalar.activation(out=squares[:], in_=y_ps[b][:, i, :], func=ACT.Square, accum_out=ssq[:, n : n + 1])
-
-        def inverse_root(src, n0, n, dst0):
-            nc.scalar.activation(
-                out=rstd[:, dst0 : dst0 + n],
-                in_=src[:, n0 : n0 + n],
-                func=ACT.Abs_reciprocal_sqrt,
-                scale=1.0 / E,
-                bias=EPS,
-            )
-
-        def moments(c):
-            for g in range(0, H, 2):
-                u = H * c + g
+        def bank_moments(b):
+            for i in range(0, BANK_UNITS, 2):
+                col = BANK_UNITS * b + i
                 nc.vector.bn_stats(
-                    out=bn[:, u : u + 2, :].rearrange("p u k -> p (u k)"),
-                    in_=y_ps[c][:, g : g + 2, :].rearrange("p g e -> p e g"),
+                    out=moments[:, col : col + 2, :].rearrange("p u k -> p (u k)"),
+                    in_=y_ps[b][:, i : i + 2, :].rearrange("p u e -> p e u"),
                 )
 
         def square_means():
-            nc.vector.tensor_tensor(out=mean_sq[:], in0=bn[:, :, 1], in1=bn[:, :, 1], op=ALU.mult)
+            nc.vector.tensor_tensor(out=mean_sq[:], in0=moments[:, :, 1], in1=moments[:, :, 1], op=ALU.mult)
 
         def join_moments():
             nc.vector.scalar_tensor_tensor(
-                out=ssq_v[:], in0=mean_sq[:], scalar=float(E), in1=bn[:, :, 2], op0=ALU.mult, op1=ALU.add
+                out=sum_sq_early[:], in0=mean_sq[:], scalar=float(E), in1=moments[:, :, 2], op0=ALU.mult, op1=ALU.add
+            )
+
+        def inverse_rms(sum_sq, cols):
+            nc.scalar.activation(
+                out=inv_rms[:, cols], in_=sum_sq[:, cols], func=ACT.Abs_reciprocal_sqrt, scale=1.0 / E, bias=EPS
             )
 
         def normalise(b, i):
-            n = 4 * b + i
+            col = BANK_UNITS * b + i
             nc.vector.scalar_tensor_tensor(
                 out=o_sb[b][:, i, :],
                 in0=y_ps[b][:, i, :],
-                scalar=rstd[:, n : n + 1],
+                scalar=inv_rms[:, col : col + 1],
                 in1=gn_sb[:],
                 op0=ALU.mult,
                 op1=ALU.mult,
@@ -212,96 +244,65 @@ def tile_rows_a_silu_mask_cap_onorm_kernel(tc, qT, kT, t, v, mask, gn, out):
                 src = o_sb[b][:, i0 : i0 + n, :]
             else:
                 g0 = 2 * (b - 2) + i0 // 2
-                dst = out[g0 : g0 + n // 2, 2 * QC : NQ, :].rearrange("h (m i) e -> m h (i e)", i=2)
-                src = o_sb[b][:, i0 : i0 + n, :].rearrange("p (h i) e -> p h (i e)", i=2)
+                dst = out[g0 : g0 + n // 2, 2 * QC : NQ, :].rearrange("h (m x) e -> m h (x e)", x=2)
+                src = o_sb[b][:, i0 : i0 + n, :].rearrange("p (h x) e -> p h (x e)", x=2)
             nc.sync.dma_start(out=dst, in_=src)
 
-        dst, src = k_views(0, 0, P)
-        nc.vector.tensor_copy(out=dst, in_=src)
-        dst, src = k_views(1, 0, P)
-        nc.scalar.copy(out=dst, in_=src)
-        dst, src = q_views(q_bf0, q_raw0)
-        nc.vector.tensor_copy(out=dst, in_=src)
-        dst, src = q_views(q_bf1, q_raw1)
-        nc.scalar.copy(out=dst, in_=src)
-        k_quantize(0)
-        quantize(q_codes[:, 0:QC], q_scales[:, 0:QC], q_bf0[:].rearrange("p q j -> p (q j)"))
+        round_keys(nc.vector.tensor_copy, 0)
+        round_keys(nc.scalar.copy, 1)
+        round_queries(nc.vector.tensor_copy, 0)
+        round_queries(nc.scalar.copy, 1)
+        quantize_keys(0)
+        quantize_queries(0)
         for r in range(1, PACK):
-            k_quantize(r)
+            quantize_keys(r)
         for u in range(H):
             scores(u)
-        quantize(q_codes[:, QC : 2 * QC], q_scales[:, QC : 2 * QC], q_bf1[:].rearrange("p q j -> p (q j)"))
-        mask_scale(0)
-        nc.vector.tensor_copy(
-            out=q_bf2[:].rearrange("p (i m) j -> p m j i", i=2), in_=q_raw2[:].rearrange("p j (m i) -> p m j i", i=2)
-        )
-        mask_scale(1)
-        quantize(q_codes[:, 2 * QC : NQ], q_scales[:, 2 * QC : NQ], q_bf2[:].rearrange("p q j -> p (q j)"))
+        quantize_queries(1)
+        scale_mask(0)
+        round_late_queries()
 
-        cap(0)
-        cap(1)
-        cap(2)
-        silu(0, 2)
-        weigh(0, 2)
-        nc.vector.tensor_copy(
-            out=v_bf[:].rearrange("p h (c i) r -> p h c r i", i=4),
-            in_=v_raw[:].rearrange("p h (r c i) -> p h c r i", r=PACK, i=4),
-        )
-        cap(3)
-        cap(4)
-        silu(2, 2)
-        weigh(2, 2)
-        quantize(v_codes[:], v_scales[:], v_bf[:].rearrange("p h e r -> p (h e r)"))
-        w_quantize(0, 4)
-        cap(5)
-        cap(6)
-        values(0, 4)
-        silu(4, 2)
-        weigh(4, 2)
-        cap(7)
-        cap(8)
-        silu(6, 2)
-        weigh(6, 2)
-        moments(0)
-        w_quantize(4, 4)
-        cap(9)
-        cap(10)
-        silu(8, 2)
-        weigh(8, 2)
-        cap(11)
-        values(4, 4)
-        cap(12)
-        silu(10, 2)
-        weigh(10, 2)
-        moments(1)
-        w_quantize(8, 4)
-        values(8, 4)
-        cap(13)
-        cap(14)
-        silu(12, 2)
-        cap(15)
-        silu(14, 1)
-        silu(15, 1)
-        square_means()
-        weigh(12, 2)
-        join_moments()
-        weigh(14, 1)
-        w_quantize(12, 2)
-        values(12, 2)
-        weigh(15, 1)
-        w_quantize(14, 1)
-        values(14, 1)
-        w_quantize(15, 1)
-        values(15, 1)
-        inverse_root(ssq_v, 0, 2 * H, 0)
+        after = {
+            0: [quantize_late_queries],
+            1: [lambda: scale_mask(1)],
+            2: [round_values],
+            3: [quantize_values, lambda: quantize_weights(0, H)],
+            4: [lambda: results(0, H)],
+            6: [lambda: bank_moments(0), lambda: quantize_weights(H, H)],
+            8: [lambda: results(H, H)],
+            10: [lambda: bank_moments(1), lambda: quantize_weights(2 * H, H), lambda: results(2 * H, H), square_means],
+            12: [join_moments],
+            14: [lambda: quantize_weights(12, 2), lambda: results(12, 2)],
+            15: [
+                lambda: quantize_weights(14, 1),
+                lambda: results(14, 1),
+                lambda: quantize_weights(15, 1),
+                lambda: results(15, 1),
+            ],
+        }
+
+        next_cap = 0
+        for u, n in GROUPS:
+            for ahead in range(next_cap, min(u + n + 1, UNITS)):
+                cap(ahead)
+            next_cap = min(u + n + 1, UNITS)
+            silu(u, n)
+            weigh(u, n)
+            for step in after[u]:
+                step()
+
+        inverse_rms(sum_sq_early, slice(0, 2 * BANK_UNITS))
         for b in (2, 3):
-            for i in range(4):
-                square_sum(b, i)
-            inverse_root(ssq, 4 * b, 4, 4 * b)
-        for b in range(4):
-            for i in range(4):
+            for i in range(BANK_UNITS):
+                col = BANK_UNITS * b + i
+                nc.scalar.activation(
+                    out=squares[:], in_=y_ps[b][:, i, :], func=ACT.Square, accum_out=sum_sq_late[:, col : col + 1]
+                )
+            inverse_rms(sum_sq_late, slice(BANK_UNITS * b, BANK_UNITS * (b + 1)))
+
+        for b in range(CHUNKS):
+            piece = BANK_UNITS // 2 if b in (0, CHUNKS - 1) else BANK_UNITS
+            for i in range(BANK_UNITS):
                 normalise(b, i)
-                if b in (0, 3) and i % 2 == 1:
-                    store(b, i - 1, 2)
-            if b in (1, 2):
-                store(b, 0, 4)
+                if (i + 1) % piece == 0:
+                    store(b, i + 1 - piece, piece)

from contextlib import ExitStack

import concourse.mybir as mybir

F32 = mybir.dt.float32
BF16 = mybir.dt.bfloat16
U32 = mybir.dt.uint32
U8 = mybir.dt.uint8
FP8X4 = mybir.dt.float8_e4m3fn_x4
ACT = mybir.ActivationFunctionType
ALU = mybir.AluOpType

H, D, NQ, N, E = 4, 128, 512, 512, 128
P = 128
PACK = 4
ROWS = D // PACK
QC = 128
CHUNKS = NQ // QC
UNITS = H * CHUNKS
BANK_UNITS = 4
CAP = 2.0
EPS = 16 * 16 * 1e-5
FLOPS = 2 * H * NQ * N * (D + E)

GROUPS = [(u, 1) for u in range(H)] + [(u, 2) for u in range(H, UNITS - 2, 2)] + [(UNITS - 2, 1), (UNITS - 1, 1)]


def result_place(u):
    c, g = divmod(u, H)
    if c < 2:
        return c, g
    return 2 + g // 2, 2 * (g % 2) + c - 2


def tile_rows_a_silu_mask_cap_onorm_kernel(tc, qT, kT, t, v, mask, gn, out):
    nc = tc.nc
    with ExitStack() as ctx:
        sb = ctx.enter_context(tc.tile_pool(name="sb", bufs=1))
        ps = ctx.enter_context(tc.psum_pool(name="ps", bufs=1))
        ctx.enter_context(tc.manual_schedule())

        def sbuf(name, shape, dtype):
            return sb.tile(shape, dtype, name=name, align_bytes=64)

        q_hbm = qT.rearrange("h (p j) q -> (h p) j q", j=PACK)
        mask_hbm = mask.rearrange("(s r) q -> s r q", r=PACK)
        k_raw = sbuf("k_raw", [P, PACK, N], F32)
        q_raw = [sbuf("q_raw%d" % c, [P, PACK, QC], F32) for c in range(2)]
        q_raw_late = sbuf("q_raw_late", [P, PACK, 2 * QC], F32)
        mask_raw = [sbuf("mask_raw%d" % half, [P, PACK, 2 * QC], F32) for half in range(2)]
        v_raw = sbuf("v_raw", [P, H, PACK * E], F32)
        t_sb = sbuf("t_sb", [P, PACK], F32)
        gn_sb = sbuf("gn_sb", [P, E], F32)
        nc.sync.dma_start(out=k_raw[:], in_=kT.rearrange("h (p j) n -> (h p) j n", j=PACK))
        nc.sync.dma_start(out=q_raw[0][:], in_=q_hbm[:, :, 0:QC])
        nc.scalar.dma_start(out=t_sb[:], in_=t.rearrange("(s r) o -> s (r o)", r=PACK))
        nc.sync.dma_start(out=q_raw[1][:], in_=q_hbm[:, :, QC : 2 * QC])
        nc.sync.dma_start(out=mask_raw[0][:], in_=mask_hbm[:, :, 0 : 2 * QC])
        nc.sync.dma_start(out=q_raw_late[:], in_=q_hbm[:, :, 2 * QC : NQ])
        nc.sync.dma_start(out=mask_raw[1][:], in_=mask_hbm[:, :, 2 * QC : NQ])
        nc.sync.dma_start(out=v_raw[:], in_=v.rearrange("h (s r) e -> s h (r e)", r=PACK))
        nc.sync.dma_start(out=gn_sb[:], in_=gn)

        zero_in = sbuf("zero_in", [P, 1], F32)
        zero_bias = sbuf("zero_bias", [P, 1], F32)
        nc.vector.memset(zero_in[:], 0.0)
        nc.scalar.activation(out=zero_bias[:], in_=zero_in[:], func=ACT.Silu)

        k_bf = [sbuf("k_bf%d" % half, [P, 2, P, PACK], BF16) for half in range(2)]
        k_codes = sbuf("k_codes", [P, N], U32)
        k_scales = sbuf("k_scales", [P, N], U8)
        q_bf = [sbuf("q_bf%d" % c, [P, QC, PACK], BF16) for c in range(2)]
        q_bf_late = sbuf("q_bf_late", [P, 2 * QC, PACK], BF16)
        q_codes = sbuf("q_codes", [P, NQ], U32)
        q_scales = sbuf("q_scales", [P, NQ], U8)
        v_bf = sbuf("v_bf", [P, H, E, PACK], BF16)
        v_codes = sbuf("v_codes", [P, H * E], U32)
        v_scales = sbuf("v_scales", [P, H * E], U8)
        mask_t = [sbuf("mask_t%d" % half, [P, 2 * QC, PACK], F32) for half in range(2)]
        capped = [sbuf("capped%d" % c, [P, H, QC * PACK], F32) for c in range(CHUNKS)]
        silus = [sbuf("silus%d" % c, [P, H, QC * PACK], F32) for c in range(CHUNKS)]
        w_bf = [sbuf("w_bf%d" % c, [P, H, QC * PACK], BF16) for c in range(CHUNKS)]
        w_codes = [sbuf("w_codes%d" % c, [P, H * QC], U32) for c in range(CHUNKS)]
        w_scales = [sbuf("w_scales%d" % c, [P, H * QC], U8) for c in range(CHUNKS)]
        squares = sbuf("squares", [P, E], BF16)
        moments = sbuf("moments", [P, 2 * BANK_UNITS, 3], F32)
        mean_sq = sbuf("mean_sq", [P, 2 * BANK_UNITS], F32)
        sum_sq_early = sbuf("sum_sq_early", [P, 2 * BANK_UNITS], F32)
        sum_sq_late = sbuf("sum_sq_late", [P, UNITS], F32)
        inv_rms = sbuf("inv_rms", [P, UNITS], F32)
        o_sb = [sbuf("o_sb%d" % b, [P, BANK_UNITS, E], F32) for b in range(CHUNKS)]
        s_ps = [ps.tile([P, PACK, QC], F32, name="s_ps%d" % g) for g in range(H)]
        y_ps = [ps.tile([P, BANK_UNITS, E], F32, name="y_ps%d" % b) for b in range(CHUNKS)]

        def quantize(codes, scales, values):
            nc.vector.quantize_mx(out=codes.bitcast(FP8X4), scales=scales, in_=values)

        def round_keys(copy, half):
            src = k_raw[:].rearrange("p j (s r) -> p s j r", r=PACK)[:, :, :, 2 * half : 2 * half + 2]
            copy(out=k_bf[half][:].rearrange("p r s j -> p s j r"), in_=src)

        def quantize_keys(r):
            cols = slice(P * r, P * (r + 1))
            quantize(k_codes[:, cols], k_scales[:, cols], k_bf[r // 2][:, r % 2, :, :].rearrange("p s j -> p (s j)"))

        def round_queries(copy, c):
            copy(
                out=q_bf[c][:].rearrange("p (m x) j -> p m j x", x=4),
                in_=q_raw[c][:].rearrange("p j (m x) -> p m j x", x=4),
            )

        def quantize_queries(c):
            cols = slice(QC * c, QC * (c + 1))
            quantize(q_codes[:, cols], q_scales[:, cols], q_bf[c][:].rearrange("p q j -> p (q j)"))

        def round_late_queries():
            nc.vector.tensor_copy(
                out=q_bf_late[:].rearrange("p (x m) j -> p m j x", x=2),
                in_=q_raw_late[:].rearrange("p j (m x) -> p m j x", x=2),
            )

        def quantize_late_queries():
            cols = slice(2 * QC, NQ)
            quantize(q_codes[:, cols], q_scales[:, cols], q_bf_late[:].rearrange("p q j -> p (q j)"))

        def scale_mask(half):
            order = "p (m x) r -> p m r x" if half == 0 else "p (x m) r -> p m r x"
            nc.vector.tensor_tensor(
                out=mask_t[half][:].rearrange(order, x=2),
                in0=mask_raw[half][:].rearrange("p r (m x) -> p m r x", x=2),
                in1=t_sb[:].unsqueeze(1).unsqueeze(3).to_broadcast([P, QC, PACK, 2]),
                op=ALU.mult,
            )

        def round_values():
            nc.vector.tensor_copy(
                out=v_bf[:].rearrange("p h (m x) r -> p h m r x", x=4),
                in_=v_raw[:].rearrange("p h (r m x) -> p h m r x", r=PACK, x=4),
            )

        def quantize_values():
            quantize(v_codes[:], v_scales[:], v_bf[:].rearrange("p h e r -> p (h e r)"))

        def scores(u):
            c, g = divmod(u, H)
            rows = slice(ROWS * g, ROWS * (g + 1))
            q_cols = slice(QC * c, QC * (c + 1))
            for r in range(PACK):
                k_cols = slice(P * r, P * (r + 1))
                nc.tensor.matmul_mx(
                    out=s_ps[g][:, r, :],
                    lhsT=k_codes[rows, k_cols].bitcast(FP8X4),
                    lhsT_scale=k_scales[rows, k_cols],
                    rhs=q_codes[rows, q_cols].bitcast(FP8X4),
                    rhs_scale=q_scales[rows, q_cols],
                    start=True,
                    stop=True,
                )

        def cap(u):
            c, g = divmod(u, H)
            nc.scalar.activation(
                out=capped[c][:, g, :].rearrange("p (q r) -> p q r", r=PACK),
                in_=s_ps[g][:].rearrange("p r q -> p q r"),
                func=ACT.Tanh,
                scale=1.0 / CAP,
                bias=zero_bias[:],
            )
            if u + H < UNITS:
                scores(u + H)

        def silu(u, n):
            c, g = divmod(u, H)
            nc.scalar.activation(
                out=silus[c][:, g : g + n, :], in_=capped[c][:, g : g + n, :], func=ACT.Silu, scale=CAP
            )

        def weigh(u, n):
            c, g = divmod(u, H)
            factors = mask_t[c // 2][:, QC * (c % 2) : QC * (c % 2 + 1), :].rearrange("p q r -> p (q r)")
            nc.vector.tensor_tensor(
                out=w_bf[c][:, g : g + n, :],
                in0=silus[c][:, g : g + n, :],
                in1=factors.unsqueeze(1).to_broadcast([P, n, QC * PACK]),
                op=ALU.mult,
            )

        def quantize_weights(u, n):
            c, g = divmod(u, H)
            cols = slice(QC * g, QC * (g + n))
            quantize(w_codes[c][:, cols], w_scales[c][:, cols], w_bf[c][:, g : g + n, :].rearrange("p g x -> p (g x)"))

        def results(u0, n):
            for u in range(u0, u0 + n):
                c, g = divmod(u, H)
                b, i = result_place(u)
                q_cols = slice(QC * g, QC * (g + 1))
                e_cols = slice(E * g, E * (g + 1))
                nc.tensor.matmul_mx(
                    out=y_ps[b][:, i, :],
                    lhsT=w_codes[c][:, q_cols].bitcast(FP8X4),
                    lhsT_scale=w_scales[c][:, q_cols],
                    rhs=v_codes[:, e_cols].bitcast(FP8X4),
                    rhs_scale=v_scales[:, e_cols],
                    start=True,
                    stop=True,
                )

        def bank_moments(b):
            for i in range(0, BANK_UNITS, 2):
                col = BANK_UNITS * b + i
                nc.vector.bn_stats(
                    out=moments[:, col : col + 2, :].rearrange("p u k -> p (u k)"),
                    in_=y_ps[b][:, i : i + 2, :].rearrange("p u e -> p e u"),
                )

        def square_means():
            nc.vector.tensor_tensor(out=mean_sq[:], in0=moments[:, :, 1], in1=moments[:, :, 1], op=ALU.mult)

        def join_moments():
            nc.vector.scalar_tensor_tensor(
                out=sum_sq_early[:], in0=mean_sq[:], scalar=float(E), in1=moments[:, :, 2], op0=ALU.mult, op1=ALU.add
            )

        def inverse_rms(sum_sq, cols):
            nc.scalar.activation(
                out=inv_rms[:, cols], in_=sum_sq[:, cols], func=ACT.Abs_reciprocal_sqrt, scale=1.0 / E, bias=EPS
            )

        def normalise(b, i):
            col = BANK_UNITS * b + i
            nc.vector.scalar_tensor_tensor(
                out=o_sb[b][:, i, :],
                in0=y_ps[b][:, i, :],
                scalar=inv_rms[:, col : col + 1],
                in1=gn_sb[:],
                op0=ALU.mult,
                op1=ALU.mult,
            )

        def store(b, i0, n):
            if b < 2:
                dst = out[i0 : i0 + n, QC * b : QC * (b + 1), :].rearrange("h q e -> q h e")
                src = o_sb[b][:, i0 : i0 + n, :]
            else:
                g0 = 2 * (b - 2) + i0 // 2
                dst = out[g0 : g0 + n // 2, 2 * QC : NQ, :].rearrange("h (m x) e -> m h (x e)", x=2)
                src = o_sb[b][:, i0 : i0 + n, :].rearrange("p (h x) e -> p h (x e)", x=2)
            nc.sync.dma_start(out=dst, in_=src)

        round_keys(nc.vector.tensor_copy, 0)
        round_keys(nc.scalar.copy, 1)
        round_queries(nc.vector.tensor_copy, 0)
        round_queries(nc.scalar.copy, 1)
        quantize_keys(0)
        quantize_queries(0)
        for r in range(1, PACK):
            quantize_keys(r)
        for u in range(H):
            scores(u)
        quantize_queries(1)
        scale_mask(0)
        round_late_queries()

        after = {
            0: [quantize_late_queries],
            1: [lambda: scale_mask(1)],
            2: [round_values],
            3: [quantize_values, lambda: quantize_weights(0, H)],
            4: [lambda: results(0, H)],
            6: [lambda: bank_moments(0), lambda: quantize_weights(H, H)],
            8: [lambda: results(H, H)],
            10: [lambda: bank_moments(1), lambda: quantize_weights(2 * H, H), lambda: results(2 * H, H), square_means],
            12: [join_moments],
            14: [lambda: quantize_weights(12, 2), lambda: results(12, 2)],
            15: [
                lambda: quantize_weights(14, 1),
                lambda: results(14, 1),
                lambda: quantize_weights(15, 1),
                lambda: results(15, 1),
            ],
        }

        next_cap = 0
        for u, n in GROUPS:
            for ahead in range(next_cap, min(u + n + 1, UNITS)):
                cap(ahead)
            next_cap = min(u + n + 1, UNITS)
            silu(u, n)
            weigh(u, n)
            for step in after[u]:
                step()

        inverse_rms(sum_sq_early, slice(0, 2 * BANK_UNITS))
        for b in (2, 3):
            for i in range(BANK_UNITS):
                col = BANK_UNITS * b + i
                nc.scalar.activation(
                    out=squares[:], in_=y_ps[b][:, i, :], func=ACT.Square, accum_out=sum_sq_late[:, col : col + 1]
                )
            inverse_rms(sum_sq_late, slice(BANK_UNITS * b, BANK_UNITS * (b + 1)))

        for b in range(CHUNKS):
            piece = BANK_UNITS // 2 if b in (0, CHUNKS - 1) else BANK_UNITS
            for i in range(BANK_UNITS):
                normalise(b, i)
                if (i + 1) % piece == 0:
                    store(b, i + 1 - piece, piece)
